import numpy as np
import ml_dtypes


def mxq(x, axis, fmt="e4m3"):
    dtype, down = {"e4m3": (ml_dtypes.float8_e4m3fn, 7), "e5m2": (ml_dtypes.float8_e5m2, 14)}[fmt]
    v = np.moveaxis(np.asarray(x, np.float32).astype(ml_dtypes.bfloat16).astype(np.float64), axis, -1)
    blocks = v.reshape(v.shape[:-1] + (-1, 32))
    amax = np.abs(blocks).max(-1, keepdims=True)
    byte = np.maximum(np.where(amax > 0, np.frexp(amax)[1] - 1 + 127, 0) - down, 1)
    scale = np.exp2(byte - 127.0)
    codes = (blocks / scale).astype(np.float32).astype(dtype).astype(np.float64)
    return np.moveaxis((codes * scale).reshape(v.shape), -1, axis)


WIDE = False


def mx_kscale(k):
    if not WIDE:
        return np.ones(k)
    levels = np.array([10, -10, 5, -5, 0])
    if k % 512:
        return np.exp2(np.random.permutation(np.resize(levels, k // 32))).repeat(32)
    a = np.empty((k // 512, 16))
    for p in range(k // 512):
        a[p, :8] = np.random.permutation(np.resize(levels, 8))
        for g in range(8):
            far = levels[np.abs(levels - a[p, g]) >= 10]
            a[p, g + 8] = far[np.random.randint(len(far))]
    return np.exp2(a.ravel()).repeat(32)


def f64(x):
    return np.asarray(x).astype(np.float64)


def striped(idx):
    return np.tile(np.asarray(idx).reshape(-1, 16).T, (8, 1)).astype(np.uint16)


def unstriped(offs):
    return offs[:16].T.reshape(-1).astype(np.int64)


E2M1 = np.array([0.0, 0.5, 1.0, 1.5, 2.0, 3.0, 4.0, 6.0, -0.0, -0.5, -1.0, -1.5, -2.0, -3.0, -4.0, -6.0])


def pack_weight(w, fmt):
    k, n = w.shape
    w = f64(np.asarray(w, np.float32).astype(ml_dtypes.bfloat16)).reshape(k // 32, 32, n)
    amax = np.abs(w).max(1)
    if fmt == "e4m3":
        byte = np.frexp(amax)[1] - 1 + 127 - 7
    else:
        mant, ex = np.frexp(amax / 6.0)
        byte = np.where(mant > 0.5, ex, ex - 1) + 127
    byte = np.clip(np.where(amax > 0, byte, 1), 1, 254)
    scaled = (w * np.exp2(127.0 - byte)[:, None, :]).reshape(k, n).astype(np.float32)
    by_word = np.ascontiguousarray(scaled.reshape(k // 512, 128, 4, n).transpose(0, 1, 3, 2))
    if fmt == "e4m3":
        words = by_word.astype(ml_dtypes.float8_e4m3fn).view(np.uint8)
    else:
        c = by_word.astype(ml_dtypes.float4_e2m1fn).view(np.uint8) & 0xF
        words = (c[..., 0::2] | (c[..., 1::2] << 4)).reshape(k // 512, 128, 2 * n)
    return np.ascontiguousarray(words), np.ascontiguousarray(byte.astype(np.uint8).reshape(k // 512, 16, n))


def unpack_weight(words, scales, fmt):
    g, _, n = scales.shape
    words = np.ascontiguousarray(words).reshape(g, 128, n, -1)
    if fmt == "e4m3":
        vals = words.view(ml_dtypes.float8_e4m3fn).astype(np.float64)
    else:
        nib = np.empty((g, 128, n, 4), np.uint8)
        nib[..., 0::2] = words & 0xF
        nib[..., 1::2] = words >> 4
        vals = E2M1[nib]
    vals = vals * np.repeat(np.exp2(scales.astype(np.float64) - 127.0), 8, axis=1)[..., None]
    return vals.transpose(0, 1, 3, 2).reshape(g * 512, n)


def sigmoid(v):
    return 1.0 / (1.0 + np.exp(-v))


B, N, T, D, NQ = 2, 512, 2048, 512, 128


def setup_inputs():
    n = np.random.standard_normal
    jdx = np.random.permutation(1024)[:B * NQ]
    idx = np.random.permutation(T)[:B * N]
    s = mx_kscale(D)[:, None]
    kp = pack_weight(n((D, T)) / s, "e4m3")
    return {
        "qT": (n((D, 1024)) * s * (1.00 / np.sqrt(D))).astype(np.float32),
        "k_words": kp[0],
        "k_scales": kp[1],
        "offq": striped(jdx),
        "offs": striped(idx),
    }


def reference(qT, k_words, k_scales, offq, offs):
    jdx = unstriped(offq)
    idx = unstriped(offs)
    pick = lambda x, which: x[:, which].reshape(x.shape[0], B, -1).transpose(1, 0, 2)
    qg = mxq(pick(f64(qT), jdx), 1, "e4m3")
    k = unpack_weight(k_words, k_scales, "e4m3")
    kg = pick(k, idx)
    qq = qg
    a = qq.transpose(0, 2, 1) @ kg
    y = sigmoid(a)
    out = np.zeros((B, NQ, T))
    for b in range(B):
        out[b][:, idx[b * N:(b + 1) * N]] = y[b]
    return out

@@ -1,0 +1,107 @@
+from contextlib import ExitStack
+
+import concourse.mybir as mybir
+
+F32 = mybir.dt.float32
+BF16 = mybir.dt.bfloat16
+I32 = mybir.dt.int32
+U32 = mybir.dt.uint32
+U16 = mybir.dt.uint16
+U8 = mybir.dt.uint8
+FP8X4 = mybir.dt.float8_e4m3fn_x4
+SIGMOID = mybir.ActivationFunctionType.Sigmoid
+
+B, NQ, N, T, D, QPOOL = 2, 128, 512, 2048, 512, 1024
+P = 128
+PACK = 4
+FLOPS = 2 * B * NQ * N * D
+
+
+def tile_attend_lq_scat_topk_kernel(tc, qT, k_words, k_scales, offq, offs, out):
+    nc = tc.nc
+    with ExitStack() as ctx:
+        pool = ctx.enter_context(tc.tile_pool(name="held", bufs=1))
+        psum = ctx.enter_context(tc.psum_pool(name="psum", bufs=1))
+
+        key_list = pool.tile([P, B * N // 16], U16, name="key_list")
+        query_list = pool.tile([P, B * NQ // 16], U16, name="query_list")
+        scale_pool = pool.tile([P, T // 4], I32, name="scale_pool", align_bytes=64)
+        word_pool = pool.tile([P, T], I32, name="word_pool", align_bytes=64)
+        q_rows = [pool.tile([P, QPOOL], F32, name="q_rows%d" % t) for t in range(PACK)]
+        maps = [pool.tile([P, T], F32, name="map%d" % b) for b in range(B)]
+
+        nc.vector.memset(scale_pool[:], 0)
+        nc.sync.dma_start(key_list[:], offs)
+        nc.sync.dma_start(query_list[:], offq)
+        for quad in range(4):
+            nc.scalar.dma_start(scale_pool[28 * quad : 28 * quad + 16, :], k_scales[0].bitcast(I32))
+        q_view = qT.rearrange("(p t) c -> t p c", t=PACK)
+        nc.sync.dma_start(q_rows[0][:], q_view[0])
+        nc.sync.dma_start(q_rows[1][:], q_view[1])
+        nc.sync.dma_start(word_pool[:], k_words[0].rearrange("p n t -> p (n t)").bitcast(I32))
+        nc.sync.dma_start(q_rows[2][:], q_view[2])
+        nc.sync.dma_start(q_rows[3][:], q_view[3])
+        for b in range(B):
+            nc.vector.memset(maps[b][:], 0.0)
+
+        k_codes = [pool.tile([P, N], U32, name="k_codes%d" % b, align_bytes=64) for b in range(B)]
+        k_bytes = [pool.tile([P, N], U8, name="k_bytes%d" % b, align_bytes=64) for b in range(B)]
+        q_bf = pool.tile([P, B * NQ, PACK], BF16, name="q_bf", align_bytes=64)
+        q_codes = [pool.tile([P, NQ], U32, name="q_codes%d" % b, align_bytes=64) for b in range(B)]
+        q_bytes = [pool.tile([P, NQ], U8, name="q_bytes%d" % b, align_bytes=64) for b in range(B)]
+        scores = [psum.tile([P, N], F32, name="scores%d" % b) for b in range(B)]
+        links = [pool.tile([P, N], F32, name="links%d" % b) for b in range(B)]
+
+        def keys_of(b):
+            return key_list[:, b * N // 16 : (b + 1) * N // 16]
+
+        def gather_bytes(b):
+            nc.vector.tensor_copy(k_bytes[b][:], scale_pool[:].bitcast(U8).indirect(keys_of(b)))
+
+        def gather_words(b):
+            nc.vector.tensor_copy(k_codes[b][:], word_pool[:].bitcast(U32).indirect(keys_of(b)))
+
+        def gather_rows(t, b0, b1):
+            nc.vector.tensor_copy(
+                q_bf[:, b0 * NQ : b1 * NQ, t],
+                q_rows[t][:].indirect(query_list[:, b0 * NQ // 16 : b1 * NQ // 16]),
+            )
+
+        def quantise(b):
+            nc.vector.quantize_mx(
+                out=q_codes[b][:].bitcast(FP8X4),
+                scales=q_bytes[b][:],
+                in_=q_bf[:, b * NQ : (b + 1) * NQ, :].rearrange("p c t -> p (c t)"),
+            )
+
+        def score(b):
+            nc.tensor.matmul_mx(
+                out=scores[b][:],
+                lhsT=q_codes[b][:].bitcast(FP8X4),
+                lhsT_scale=q_bytes[b][:],
+                rhs=k_codes[b][:].bitcast(FP8X4),
+                rhs_scale=k_bytes[b][:],
+                start=True,
+                stop=True,
+            )
+            nc.scalar.activation(links[b][:], scores[b][:], SIGMOID)
+
+        def scatter(b):
+            nc.vector.tensor_copy(maps[b][:].indirect(keys_of(b)), links[b][:])
+            nc.sync.dma_start(out[b], maps[b][:])
+
+        gather_bytes(0)
+        gather_bytes(1)
+        gather_rows(0, 0, B)
+        gather_rows(1, 0, B)
+        gather_words(0)
+        gather_rows(2, 0, B)
+        gather_rows(3, 0, 1)
+        gather_rows(3, 1, 2)
+        quantise(0)
+        score(0)
+        gather_words(1)
+        quantise(1)
+        score(1)
+        scatter(0)
+        scatter(1)

@@ -14,6 +14,7 @@ SIGMOID = mybir.ActivationFunctionType.Sigmoid
 B, NQ, N, T, D, QPOOL = 2, 128, 512, 2048, 512, 1024
 P = 128
 PACK = 4
+HALF = N // 2
 FLOPS = 2 * B * NQ * N * D
 
 
@@ -21,45 +22,49 @@ def tile_attend_lq_scat_topk_kernel(tc, qT, k_words, k_scales, offq, offs, out):
     nc = tc.nc
     with ExitStack() as ctx:
         pool = ctx.enter_context(tc.tile_pool(name="held", bufs=1))
+        ring = ctx.enter_context(tc.tile_pool(name="ring", bufs=2))
         psum = ctx.enter_context(tc.psum_pool(name="psum", bufs=1))
 
         key_list = pool.tile([P, B * N // 16], U16, name="key_list")
         query_list = pool.tile([P, B * NQ // 16], U16, name="query_list")
         scale_pool = pool.tile([P, T // 4], I32, name="scale_pool", align_bytes=64)
         word_pool = pool.tile([P, T], I32, name="word_pool", align_bytes=64)
-        q_rows = [pool.tile([P, QPOOL], F32, name="q_rows%d" % t) for t in range(PACK)]
         maps = [pool.tile([P, T], F32, name="map%d" % b) for b in range(B)]
+        q_view = qT.rearrange("(p t) c -> t p c", t=PACK)
 
-        nc.vector.memset(scale_pool[:], 0)
-        nc.sync.dma_start(key_list[:], offs)
+        def load_rows(t):
+            rows = ring.tile([P, QPOOL], F32, name="q_rows")
+            nc.sync.dma_start(rows[:], q_view[t])
+            return rows
+
+        nc.gpsimd.memset(scale_pool[:], 0)
         nc.sync.dma_start(query_list[:], offq)
+        nc.sync.dma_start(key_list[:], offs)
         for quad in range(4):
             nc.scalar.dma_start(scale_pool[28 * quad : 28 * quad + 16, :], k_scales[0].bitcast(I32))
-        q_view = qT.rearrange("(p t) c -> t p c", t=PACK)
-        nc.sync.dma_start(q_rows[0][:], q_view[0])
-        nc.sync.dma_start(q_rows[1][:], q_view[1])
+        q_rows = [load_rows(0), load_rows(1)]
         nc.sync.dma_start(word_pool[:], k_words[0].rearrange("p n t -> p (n t)").bitcast(I32))
-        nc.sync.dma_start(q_rows[2][:], q_view[2])
-        nc.sync.dma_start(q_rows[3][:], q_view[3])
-        for b in range(B):
-            nc.vector.memset(maps[b][:], 0.0)
+        nc.vector.memset(maps[0][:, : T // 2 - 1], 0.0)
+        nc.vector.memset(maps[0][:, T // 2 - 1 :], 0.0)
+        nc.gpsimd.memset(maps[1][:], 0.0)
 
-        k_codes = [pool.tile([P, N], U32, name="k_codes%d" % b, align_bytes=64) for b in range(B)]
         k_bytes = [pool.tile([P, N], U8, name="k_bytes%d" % b, align_bytes=64) for b in range(B)]
-        q_bf = pool.tile([P, B * NQ, PACK], BF16, name="q_bf", align_bytes=64)
+        q_f32 = pool.tile([P, 2, B * NQ], F32, name="q_f32")
+        q_bf = pool.tile([P, B * NQ, PACK], BF16, name="shared", align_bytes=64)
         q_codes = [pool.tile([P, NQ], U32, name="q_codes%d" % b, align_bytes=64) for b in range(B)]
         q_bytes = [pool.tile([P, NQ], U8, name="q_bytes%d" % b, align_bytes=64) for b in range(B)]
-        scores = [psum.tile([P, N], F32, name="scores%d" % b) for b in range(B)]
         links = [pool.tile([P, N], F32, name="links%d" % b) for b in range(B)]
 
-        def keys_of(b):
-            return key_list[:, b * N // 16 : (b + 1) * N // 16]
+        def keys_of(b, n0=0, n1=N):
+            return key_list[:, (b * N + n0) // 16 : (b * N + n1) // 16]
 
         def gather_bytes(b):
             nc.vector.tensor_copy(k_bytes[b][:], scale_pool[:].bitcast(U8).indirect(keys_of(b)))
 
-        def gather_words(b):
-            nc.vector.tensor_copy(k_codes[b][:], word_pool[:].bitcast(U32).indirect(keys_of(b)))
+        def gather_words(b, name):
+            codes = pool.tile([P, N], U32, name=name, align_bytes=64)
+            nc.vector.tensor_copy(codes[:], word_pool[:].bitcast(U32).indirect(keys_of(b)))
+            return codes
 
         def gather_rows(t, b0, b1):
             nc.vector.tensor_copy(
@@ -74,34 +79,41 @@ def tile_attend_lq_scat_topk_kernel(tc, qT, k_words, k_scales, offq, offs, out):
                 in_=q_bf[:, b * NQ : (b + 1) * NQ, :].rearrange("p c t -> p (c t)"),
             )
 
-        def score(b):
+        def score(b, codes, n0, n1):
+            scores = psum.tile([P, n1 - n0], F32, name="scores%d_%d" % (b, n0))
             nc.tensor.matmul_mx(
-                out=scores[b][:],
+                out=scores[:],
                 lhsT=q_codes[b][:].bitcast(FP8X4),
                 lhsT_scale=q_bytes[b][:],
-                rhs=k_codes[b][:].bitcast(FP8X4),
-                rhs_scale=k_bytes[b][:],
+                rhs=codes[:, n0:n1].bitcast(FP8X4),
+                rhs_scale=k_bytes[b][:, n0:n1],
                 start=True,
                 stop=True,
             )
-            nc.scalar.activation(links[b][:], scores[b][:], SIGMOID)
+            nc.scalar.activation(links[b][:, n0:n1], scores[:], SIGMOID)
 
-        def scatter(b):
-            nc.vector.tensor_copy(maps[b][:].indirect(keys_of(b)), links[b][:])
-            nc.sync.dma_start(out[b], maps[b][:])
+        def scatter(b, n0, n1):
+            nc.vector.tensor_copy(maps[b][:].indirect(keys_of(b, n0, n1)), links[b][:, n0:n1])
 
+        nc.vector.tensor_copy(q_f32[:, 0, :], q_rows[0][:].indirect(query_list[:]))
+        q_rows.append(load_rows(2))
+        nc.vector.tensor_copy(q_f32[:, 1, :], q_rows[1][:].indirect(query_list[:]))
+        q_rows.append(load_rows(3))
+        nc.scalar.copy(q_bf[:, :, 0:2], q_f32[:].rearrange("p t c -> p c t"))
         gather_bytes(0)
         gather_bytes(1)
-        gather_rows(0, 0, B)
-        gather_rows(1, 0, B)
-        gather_words(0)
+        codes0 = gather_words(0, "k_codes0")
         gather_rows(2, 0, B)
         gather_rows(3, 0, 1)
         gather_rows(3, 1, 2)
         quantise(0)
-        score(0)
-        gather_words(1)
         quantise(1)
-        score(1)
-        scatter(0)
-        scatter(1)
+        score(0, codes0, 0, HALF)
+        score(0, codes0, HALF, N)
+        codes1 = gather_words(1, "shared")
+        score(1, codes1, 0, N)
+        scatter(0, 0, HALF)
+        scatter(0, HALF, N)
+        nc.sync.dma_start(out[0], maps[0][:])
+        scatter(1, 0, N)
+        nc.sync.dma_start(out[1], maps[1][:])

@@ -22,7 +22,6 @@ def tile_attend_lq_scat_topk_kernel(tc, qT, k_words, k_scales, offq, offs, out):
     nc = tc.nc
     with ExitStack() as ctx:
         pool = ctx.enter_context(tc.tile_pool(name="held", bufs=1))
-        ring = ctx.enter_context(tc.tile_pool(name="ring", bufs=2))
         psum = ctx.enter_context(tc.psum_pool(name="psum", bufs=1))
 
         key_list = pool.tile([P, B * N // 16], U16, name="key_list")
@@ -33,24 +32,28 @@ def tile_attend_lq_scat_topk_kernel(tc, qT, k_words, k_scales, offq, offs, out):
         q_view = qT.rearrange("(p t) c -> t p c", t=PACK)
 
         def load_rows(t):
-            rows = ring.tile([P, QPOOL], F32, name="q_rows")
+            rows = pool.tile([P, QPOOL], F32, name="q_rows%d" % t)
             nc.sync.dma_start(rows[:], q_view[t])
             return rows
 
-        nc.gpsimd.memset(scale_pool[:], 0)
+        nc.vector.memset(scale_pool[:, :255], 0)
+        nc.vector.memset(scale_pool[:, 255:], 0)
+        q_rows = [load_rows(0)]
         nc.sync.dma_start(query_list[:], offq)
         nc.sync.dma_start(key_list[:], offs)
         for quad in range(4):
-            nc.scalar.dma_start(scale_pool[28 * quad : 28 * quad + 16, :], k_scales[0].bitcast(I32))
-        q_rows = [load_rows(0), load_rows(1)]
+            nc.sync.dma_start(scale_pool[28 * quad : 28 * quad + 16, :], k_scales[0].bitcast(I32))
         nc.sync.dma_start(word_pool[:], k_words[0].rearrange("p n t -> p (n t)").bitcast(I32))
+        q_rows.append(load_rows(1))
+        q_rows.append(load_rows(2))
+        q_rows.append(load_rows(3))
         nc.vector.memset(maps[0][:, : T // 2 - 1], 0.0)
         nc.vector.memset(maps[0][:, T // 2 - 1 :], 0.0)
         nc.gpsimd.memset(maps[1][:], 0.0)
 
         k_bytes = [pool.tile([P, N], U8, name="k_bytes%d" % b, align_bytes=64) for b in range(B)]
-        q_f32 = pool.tile([P, 2, B * NQ], F32, name="q_f32")
-        q_bf = pool.tile([P, B * NQ, PACK], BF16, name="shared", align_bytes=64)
+        q_f32 = pool.tile([P, 2, B * NQ], F32, name="shared", align_bytes=64)
+        q_bf = pool.tile([P, B * NQ, PACK], BF16, name="q_bf", align_bytes=64)
         q_codes = [pool.tile([P, NQ], U32, name="q_codes%d" % b, align_bytes=64) for b in range(B)]
         q_bytes = [pool.tile([P, NQ], U8, name="q_bytes%d" % b, align_bytes=64) for b in range(B)]
         links = [pool.tile([P, N], F32, name="links%d" % b) for b in range(B)]
@@ -96,13 +99,11 @@ def tile_attend_lq_scat_topk_kernel(tc, qT, k_words, k_scales, offq, offs, out):
             nc.vector.tensor_copy(maps[b][:].indirect(keys_of(b, n0, n1)), links[b][:, n0:n1])
 
         nc.vector.tensor_copy(q_f32[:, 0, :], q_rows[0][:].indirect(query_list[:]))
-        q_rows.append(load_rows(2))
-        nc.vector.tensor_copy(q_f32[:, 1, :], q_rows[1][:].indirect(query_list[:]))
-        q_rows.append(load_rows(3))
-        nc.scalar.copy(q_bf[:, :, 0:2], q_f32[:].rearrange("p t c -> p c t"))
         gather_bytes(0)
         gather_bytes(1)
         codes0 = gather_words(0, "k_codes0")
+        nc.vector.tensor_copy(q_f32[:, 1, :], q_rows[1][:].indirect(query_list[:]))
+        nc.scalar.copy(q_bf[:, :, 0:2], q_f32[:].rearrange("p t c -> p c t"))
         gather_rows(2, 0, B)
         gather_rows(3, 0, 1)
         gather_rows(3, 1, 2)
@@ -112,8 +113,7 @@ def tile_attend_lq_scat_topk_kernel(tc, qT, k_words, k_scales, offq, offs, out):
         score(0, codes0, HALF, N)
         codes1 = gather_words(1, "shared")
         score(1, codes1, 0, N)
-        scatter(0, 0, HALF)
-        scatter(0, HALF, N)
+        scatter(0, 0, N)
         nc.sync.dma_start(out[0], maps[0][:])
         scatter(1, 0, N)
         nc.sync.dma_start(out[1], maps[1][:])

@@ -10,6 +10,7 @@ U16 = mybir.dt.uint16
 U8 = mybir.dt.uint8
 FP8X4 = mybir.dt.float8_e4m3fn_x4
 SIGMOID = mybir.ActivationFunctionType.Sigmoid
+COPY = mybir.ActivationFunctionType.Copy
 
 B, NQ, N, T, D, QPOOL = 2, 128, 512, 2048, 512, 1024
 P = 128
@@ -28,92 +29,74 @@ def tile_attend_lq_scat_topk_kernel(tc, qT, k_words, k_scales, offq, offs, out):
         query_list = pool.tile([P, B * NQ // 16], U16, name="query_list")
         scale_pool = pool.tile([P, T // 4], I32, name="scale_pool", align_bytes=64)
         word_pool = pool.tile([P, T], I32, name="word_pool", align_bytes=64)
+        q_pool = pool.tile([P, PACK, QPOOL], F32, name="q_pool")
         maps = [pool.tile([P, T], F32, name="map%d" % b) for b in range(B)]
-        q_view = qT.rearrange("(p t) c -> t p c", t=PACK)
-
-        def load_rows(t):
-            rows = pool.tile([P, QPOOL], F32, name="q_rows%d" % t)
-            nc.sync.dma_start(rows[:], q_view[t])
-            return rows
+        q_view = qT.rearrange("(p t) c -> p t c", t=PACK)
 
         nc.vector.memset(scale_pool[:, :255], 0)
         nc.vector.memset(scale_pool[:, 255:], 0)
-        q_rows = [load_rows(0)]
+        nc.sync.dma_start(q_pool[:, 0, :], q_view[:, 0, :])
         nc.sync.dma_start(query_list[:], offq)
         nc.sync.dma_start(key_list[:], offs)
         for quad in range(4):
             nc.sync.dma_start(scale_pool[28 * quad : 28 * quad + 16, :], k_scales[0].bitcast(I32))
+        nc.sync.dma_start(q_pool[:, 1:3, :], q_view[:, 1:3, :])
+        nc.sync.dma_start(q_pool[:, 3, :], q_view[:, 3, :])
         nc.sync.dma_start(word_pool[:], k_words[0].rearrange("p n t -> p (n t)").bitcast(I32))
-        q_rows.append(load_rows(1))
-        q_rows.append(load_rows(2))
-        q_rows.append(load_rows(3))
         nc.vector.memset(maps[0][:, : T // 2 - 1], 0.0)
         nc.vector.memset(maps[0][:, T // 2 - 1 :], 0.0)
+        warm_in = pool.tile([P, 8], F32, name="warm_in")
+        warm_out = pool.tile([P, 8], F32, name="warm_out")
+        nc.gpsimd.memset(warm_in[:], 0.0)
+        nc.scalar.activation(warm_out[:], warm_in[:], SIGMOID)
         nc.gpsimd.memset(maps[1][:], 0.0)
 
-        k_bytes = [pool.tile([P, N], U8, name="k_bytes%d" % b, align_bytes=64) for b in range(B)]
-        q_f32 = pool.tile([P, 2, B * NQ], F32, name="shared", align_bytes=64)
+        k_bytes = pool.tile([P, B * N], U8, name="k_bytes", align_bytes=64)
+        k_codes = [pool.tile([P, N], U32, name="k_codes%d" % b, align_bytes=64) for b in range(B)]
+        q_cast = [pool.tile([P, QPOOL], BF16, name="q_cast%d" % t) for t in range(2)]
         q_bf = pool.tile([P, B * NQ, PACK], BF16, name="q_bf", align_bytes=64)
-        q_codes = [pool.tile([P, NQ], U32, name="q_codes%d" % b, align_bytes=64) for b in range(B)]
-        q_bytes = [pool.tile([P, NQ], U8, name="q_bytes%d" % b, align_bytes=64) for b in range(B)]
+        q_codes = pool.tile([P, B * NQ], U32, name="q_codes", align_bytes=64)
+        q_bytes = pool.tile([P, B * NQ], U8, name="q_bytes", align_bytes=64)
         links = [pool.tile([P, N], F32, name="links%d" % b) for b in range(B)]
 
-        def keys_of(b, n0=0, n1=N):
+        def keys_of(b, n0, n1):
             return key_list[:, (b * N + n0) // 16 : (b * N + n1) // 16]
 
-        def gather_bytes(b):
-            nc.vector.tensor_copy(k_bytes[b][:], scale_pool[:].bitcast(U8).indirect(keys_of(b)))
+        def gather_words(b, n0, n1):
+            nc.vector.tensor_copy(k_codes[b][:, n0:n1], word_pool[:].bitcast(U32).indirect(keys_of(b, n0, n1)))
 
-        def gather_words(b, name):
-            codes = pool.tile([P, N], U32, name=name, align_bytes=64)
-            nc.vector.tensor_copy(codes[:], word_pool[:].bitcast(U32).indirect(keys_of(b)))
-            return codes
-
-        def gather_rows(t, b0, b1):
-            nc.vector.tensor_copy(
-                q_bf[:, b0 * NQ : b1 * NQ, t],
-                q_rows[t][:].indirect(query_list[:, b0 * NQ // 16 : b1 * NQ // 16]),
-            )
-
-        def quantise(b):
-            nc.vector.quantize_mx(
-                out=q_codes[b][:].bitcast(FP8X4),
-                scales=q_bytes[b][:],
-                in_=q_bf[:, b * NQ : (b + 1) * NQ, :].rearrange("p c t -> p (c t)"),
-            )
-
-        def score(b, codes, n0, n1):
+        def score(b, n0, n1):
             scores = psum.tile([P, n1 - n0], F32, name="scores%d_%d" % (b, n0))
             nc.tensor.matmul_mx(
                 out=scores[:],
-                lhsT=q_codes[b][:].bitcast(FP8X4),
-                lhsT_scale=q_bytes[b][:],
-                rhs=codes[:, n0:n1].bitcast(FP8X4),
-                rhs_scale=k_bytes[b][:, n0:n1],
+                lhsT=q_codes[:, b * NQ : (b + 1) * NQ].bitcast(FP8X4),
+                lhsT_scale=q_bytes[:, b * NQ : (b + 1) * NQ],
+                rhs=k_codes[b][:, n0:n1].bitcast(FP8X4),
+                rhs_scale=k_bytes[:, b * N + n0 : b * N + n1],
                 start=True,
                 stop=True,
             )
             nc.scalar.activation(links[b][:, n0:n1], scores[:], SIGMOID)
 
-        def scatter(b, n0, n1):
-            nc.vector.tensor_copy(maps[b][:].indirect(keys_of(b, n0, n1)), links[b][:, n0:n1])
+        def scatter(b):
+            nc.vector.tensor_copy(maps[b][:].indirect(keys_of(b, 0, N)), links[b][:])
+            nc.sync.dma_start(out[b], maps[b][:])
 
-        nc.vector.tensor_copy(q_f32[:, 0, :], q_rows[0][:].indirect(query_list[:]))
-        gather_bytes(0)
-        gather_bytes(1)
-        codes0 = gather_words(0, "k_codes0")
-        nc.vector.tensor_copy(q_f32[:, 1, :], q_rows[1][:].indirect(query_list[:]))
-        nc.scalar.copy(q_bf[:, :, 0:2], q_f32[:].rearrange("p t c -> p c t"))
-        gather_rows(2, 0, B)
-        gather_rows(3, 0, 1)
-        gather_rows(3, 1, 2)
-        quantise(0)
-        quantise(1)
-        score(0, codes0, 0, HALF)
-        score(0, codes0, HALF, N)
-        codes1 = gather_words(1, "shared")
-        score(1, codes1, 0, N)
-        scatter(0, 0, N)
-        nc.sync.dma_start(out[0], maps[0][:])
-        scatter(1, 0, N)
-        nc.sync.dma_start(out[1], maps[1][:])
+        nc.vector.tensor_copy(k_bytes[:], scale_pool[:].bitcast(U8).indirect(key_list[:]))
+        for t in (0, 1):
+            nc.scalar.activation(q_cast[t][:], q_pool[:, t, :], COPY)
+            nc.scalar.activation(q_bf[:, :, t], q_cast[t][:].indirect(query_list[:]), COPY)
+        for t in (2, 3):
+            nc.vector.tensor_copy(q_bf[:, :, t], q_pool[:, t, :].indirect(query_list[:]))
+        nc.vector.quantize_mx(
+            out=q_codes[:].bitcast(FP8X4), scales=q_bytes[:], in_=q_bf[:].rearrange("p c t -> p (c t)")
+        )
+        gather_words(0, 0, HALF)
+        score(0, 0, HALF)
+        gather_words(0, HALF, N)
+        score(0, HALF, HALF + 128)
+        score(0, HALF + 128, N)
+        gather_words(1, 0, N)
+        score(1, 0, N)
+        scatter(0)
+        scatter(1)

@@ -38,8 +38,8 @@ def tile_attend_lq_scat_topk_kernel(tc, qT, k_words, k_scales, offq, offs, out):
         nc.sync.dma_start(q_pool[:, 0, :], q_view[:, 0, :])
         nc.sync.dma_start(query_list[:], offq)
         nc.sync.dma_start(key_list[:], offs)
-        for quad in range(4):
-            nc.sync.dma_start(scale_pool[28 * quad : 28 * quad + 16, :], k_scales[0].bitcast(I32))
+        for r in range(4):
+            nc.sync.dma_start(scale_pool[r:P:32, :], k_scales[0].bitcast(I32)[r:16:4, :])
         nc.sync.dma_start(q_pool[:, 1:3, :], q_view[:, 1:3, :])
         nc.sync.dma_start(q_pool[:, 3, :], q_view[:, 3, :])
         nc.sync.dma_start(word_pool[:], k_words[0].rearrange("p n t -> p (n t)").bitcast(I32))

@@ -38,8 +38,7 @@ def tile_attend_lq_scat_topk_kernel(tc, qT, k_words, k_scales, offq, offs, out):
         nc.sync.dma_start(q_pool[:, 0, :], q_view[:, 0, :])
         nc.sync.dma_start(query_list[:], offq)
         nc.sync.dma_start(key_list[:], offs)
-        for r in range(4):
-            nc.sync.dma_start(scale_pool[r:P:32, :], k_scales[0].bitcast(I32)[r:16:4, :])
+        nc.sync.dma_start(scale_pool[4:P:8, :], k_scales[0].bitcast(I32))
         nc.sync.dma_start(q_pool[:, 1:3, :], q_view[:, 1:3, :])
         nc.sync.dma_start(q_pool[:, 3, :], q_view[:, 3, :])
         nc.sync.dma_start(word_pool[:], k_words[0].rearrange("p n t -> p (n t)").bitcast(I32))
@@ -49,12 +48,13 @@ def tile_attend_lq_scat_topk_kernel(tc, qT, k_words, k_scales, offq, offs, out):
         warm_out = pool.tile([P, 8], F32, name="warm_out")
         nc.gpsimd.memset(warm_in[:], 0.0)
         nc.scalar.activation(warm_out[:], warm_in[:], SIGMOID)
+        k_bytes = []
         nc.gpsimd.memset(maps[1][:], 0.0)
 
-        k_bytes = pool.tile([P, B * N], U8, name="k_bytes", align_bytes=64)
+        k_picked = pool.tile([P, B * N], U8, name="k_picked", align_bytes=64)
         k_codes = [pool.tile([P, N], U32, name="k_codes%d" % b, align_bytes=64) for b in range(B)]
-        q_cast = [pool.tile([P, QPOOL], BF16, name="q_cast%d" % t) for t in range(2)]
-        q_bf = pool.tile([P, B * NQ, PACK], BF16, name="q_bf", align_bytes=64)
+        q_cast = [pool.tile([P, QPOOL], BF16, name="q_cast%d" % t, tag="cast%d" % t, align_bytes=64) for t in range(2)]
+        q_bf = pool.tile([P, B * NQ, PACK], BF16, name="q_bf", tag="woven", align_bytes=64)
         q_codes = pool.tile([P, B * NQ], U32, name="q_codes", align_bytes=64)
         q_bytes = pool.tile([P, B * NQ], U8, name="q_bytes", align_bytes=64)
         links = [pool.tile([P, N], F32, name="links%d" % b) for b in range(B)]
@@ -72,7 +72,7 @@ def tile_attend_lq_scat_topk_kernel(tc, qT, k_words, k_scales, offq, offs, out):
                 lhsT=q_codes[:, b * NQ : (b + 1) * NQ].bitcast(FP8X4),
                 lhsT_scale=q_bytes[:, b * NQ : (b + 1) * NQ],
                 rhs=k_codes[b][:, n0:n1].bitcast(FP8X4),
-                rhs_scale=k_bytes[:, b * N + n0 : b * N + n1],
+                rhs_scale=k_bytes[b][:, n0:n1],
                 start=True,
                 stop=True,
             )
@@ -82,15 +82,25 @@ def tile_attend_lq_scat_topk_kernel(tc, qT, k_words, k_scales, offq, offs, out):
             nc.vector.tensor_copy(maps[b][:].indirect(keys_of(b, 0, N)), links[b][:])
             nc.sync.dma_start(out[b], maps[b][:])
 
-        nc.vector.tensor_copy(k_bytes[:], scale_pool[:].bitcast(U8).indirect(key_list[:]))
+        def place_bytes(b, queue):
+            cols = slice(b * N // 4, (b + 1) * N // 4)
+            for r in range(4):
+                queue.dma_start(k_bytes[b][:].bitcast(I32)[r:P:32, :], k_picked[:].bitcast(I32)[4 + 8 * r : P : 32, cols])
+
+        for b in range(B):
+            nc.vector.tensor_copy(k_picked[:, b * N : (b + 1) * N], scale_pool[:].bitcast(U8).indirect(keys_of(b, 0, N)))
         for t in (0, 1):
             nc.scalar.activation(q_cast[t][:], q_pool[:, t, :], COPY)
             nc.scalar.activation(q_bf[:, :, t], q_cast[t][:].indirect(query_list[:]), COPY)
+        k_bytes.append(pool.tile([P, N], U8, name="k_bytes0", tag="cast1", align_bytes=64))
+        place_bytes(0, nc.scalar)
         for t in (2, 3):
             nc.vector.tensor_copy(q_bf[:, :, t], q_pool[:, t, :].indirect(query_list[:]))
         nc.vector.quantize_mx(
             out=q_codes[:].bitcast(FP8X4), scales=q_bytes[:], in_=q_bf[:].rearrange("p c t -> p (c t)")
         )
+        k_bytes.append(pool.tile([P, N], U8, name="k_bytes1", tag="woven", align_bytes=64))
+        place_bytes(1, nc.sync)
         gather_words(0, 0, HALF)
         score(0, 0, HALF)
         gather_words(0, HALF, N)

@@ -15,7 +15,6 @@ COPY = mybir.ActivationFunctionType.Copy
 B, NQ, N, T, D, QPOOL = 2, 128, 512, 2048, 512, 1024
 P = 128
 PACK = 4
-HALF = N // 2
 FLOPS = 2 * B * NQ * N * D
 
 
@@ -35,12 +34,11 @@ def tile_attend_lq_scat_topk_kernel(tc, qT, k_words, k_scales, offq, offs, out):
 
         nc.vector.memset(scale_pool[:, :255], 0)
         nc.vector.memset(scale_pool[:, 255:], 0)
-        nc.sync.dma_start(q_pool[:, 0, :], q_view[:, 0, :])
-        nc.sync.dma_start(query_list[:], offq)
+        nc.sync.dma_start(q_pool[:, 0:2, :], q_view[:, 0:2, :])
         nc.sync.dma_start(key_list[:], offs)
-        nc.sync.dma_start(scale_pool[4:P:8, :], k_scales[0].bitcast(I32))
-        nc.sync.dma_start(q_pool[:, 1:3, :], q_view[:, 1:3, :])
-        nc.sync.dma_start(q_pool[:, 3, :], q_view[:, 3, :])
+        nc.sync.dma_start(query_list[:], offq)
+        nc.sync.dma_start(scale_pool[0:P:8, :], k_scales[0].bitcast(I32))
+        nc.sync.dma_start(q_pool[:, 2:4, :], q_view[:, 2:4, :])
         nc.sync.dma_start(word_pool[:], k_words[0].rearrange("p n t -> p (n t)").bitcast(I32))
         nc.vector.memset(maps[0][:, : T // 2 - 1], 0.0)
         nc.vector.memset(maps[0][:, T // 2 - 1 :], 0.0)
@@ -48,22 +46,19 @@ def tile_attend_lq_scat_topk_kernel(tc, qT, k_words, k_scales, offq, offs, out):
         warm_out = pool.tile([P, 8], F32, name="warm_out")
         nc.gpsimd.memset(warm_in[:], 0.0)
         nc.scalar.activation(warm_out[:], warm_in[:], SIGMOID)
-        k_bytes = []
         nc.gpsimd.memset(maps[1][:], 0.0)
 
         k_picked = pool.tile([P, B * N], U8, name="k_picked", align_bytes=64)
+        k_bytes = [pool.tile([P, N], U8, name="k_bytes%d" % b, align_bytes=64) for b in range(B)]
         k_codes = [pool.tile([P, N], U32, name="k_codes%d" % b, align_bytes=64) for b in range(B)]
-        q_cast = [pool.tile([P, QPOOL], BF16, name="q_cast%d" % t, tag="cast%d" % t, align_bytes=64) for t in range(2)]
-        q_bf = pool.tile([P, B * NQ, PACK], BF16, name="q_bf", tag="woven", align_bytes=64)
+        q_cast = [pool.tile([P, QPOOL], BF16, name="q_cast%d" % t, align_bytes=64) for t in range(2)]
+        q_bf = pool.tile([P, B * NQ, PACK], BF16, name="q_bf", align_bytes=64)
         q_codes = pool.tile([P, B * NQ], U32, name="q_codes", align_bytes=64)
         q_bytes = pool.tile([P, B * NQ], U8, name="q_bytes", align_bytes=64)
         links = [pool.tile([P, N], F32, name="links%d" % b) for b in range(B)]
 
-        def keys_of(b, n0, n1):
-            return key_list[:, (b * N + n0) // 16 : (b * N + n1) // 16]
-
-        def gather_words(b, n0, n1):
-            nc.vector.tensor_copy(k_codes[b][:, n0:n1], word_pool[:].bitcast(U32).indirect(keys_of(b, n0, n1)))
+        def keys_of(b):
+            return key_list[:, b * N // 16 : (b + 1) * N // 16]
 
         def score(b, n0, n1):
             scores = psum.tile([P, n1 - n0], F32, name="scores%d_%d" % (b, n0))
@@ -78,35 +73,27 @@ def tile_attend_lq_scat_topk_kernel(tc, qT, k_words, k_scales, offq, offs, out):
             )
             nc.scalar.activation(links[b][:, n0:n1], scores[:], SIGMOID)
 
-        def scatter(b):
-            nc.vector.tensor_copy(maps[b][:].indirect(keys_of(b, 0, N)), links[b][:])
-            nc.sync.dma_start(out[b], maps[b][:])
-
-        def place_bytes(b, queue):
-            cols = slice(b * N // 4, (b + 1) * N // 4)
-            for r in range(4):
-                queue.dma_start(k_bytes[b][:].bitcast(I32)[r:P:32, :], k_picked[:].bitcast(I32)[4 + 8 * r : P : 32, cols])
-
         for b in range(B):
-            nc.vector.tensor_copy(k_picked[:, b * N : (b + 1) * N], scale_pool[:].bitcast(U8).indirect(keys_of(b, 0, N)))
+            nc.vector.tensor_copy(k_picked[:, b * N : (b + 1) * N], scale_pool[:].bitcast(U8).indirect(keys_of(b)))
+        nc.vector.tensor_copy(k_bytes[0][:].bitcast(I32), k_picked[:].bitcast(I32)[:, : N // 4])
+        for b in range(B):
+            cols = slice(b * N // 4, (b + 1) * N // 4)
+            for r in range(1 - b, 4):
+                nc.sync.dma_start(k_bytes[b][:].bitcast(I32)[r:P:32, :], k_picked[:].bitcast(I32)[8 * r : P : 32, cols])
         for t in (0, 1):
             nc.scalar.activation(q_cast[t][:], q_pool[:, t, :], COPY)
+        for t in (0, 1):
             nc.scalar.activation(q_bf[:, :, t], q_cast[t][:].indirect(query_list[:]), COPY)
-        k_bytes.append(pool.tile([P, N], U8, name="k_bytes0", tag="cast1", align_bytes=64))
-        place_bytes(0, nc.scalar)
         for t in (2, 3):
             nc.vector.tensor_copy(q_bf[:, :, t], q_pool[:, t, :].indirect(query_list[:]))
         nc.vector.quantize_mx(
             out=q_codes[:].bitcast(FP8X4), scales=q_bytes[:], in_=q_bf[:].rearrange("p c t -> p (c t)")
         )
-        k_bytes.append(pool.tile([P, N], U8, name="k_bytes1", tag="woven", align_bytes=64))
-        place_bytes(1, nc.sync)
-        gather_words(0, 0, HALF)
-        score(0, 0, HALF)
-        gather_words(0, HALF, N)
-        score(0, HALF, HALF + 128)
-        score(0, HALF + 128, N)
-        gather_words(1, 0, N)
+        for b in range(B):
+            nc.vector.tensor_copy(k_codes[b][:], word_pool[:].bitcast(U32).indirect(keys_of(b)))
+        for n0 in range(0, N, 128):
+            score(0, n0, n0 + 128)
         score(1, 0, N)
-        scatter(0)
-        scatter(1)
+        for b in range(B):
+            nc.vector.tensor_copy(maps[b][:].indirect(keys_of(b)), links[b][:])
+            nc.sync.dma_start(out[b], maps[b][:])

@@ -34,11 +34,12 @@ def tile_attend_lq_scat_topk_kernel(tc, qT, k_words, k_scales, offq, offs, out):
 
         nc.vector.memset(scale_pool[:, :255], 0)
         nc.vector.memset(scale_pool[:, 255:], 0)
-        nc.sync.dma_start(q_pool[:, 0:2, :], q_view[:, 0:2, :])
+        nc.sync.dma_start(q_pool[:, 0, :], q_view[:, 0, :])
         nc.sync.dma_start(key_list[:], offs)
         nc.sync.dma_start(query_list[:], offq)
         nc.sync.dma_start(scale_pool[0:P:8, :], k_scales[0].bitcast(I32))
-        nc.sync.dma_start(q_pool[:, 2:4, :], q_view[:, 2:4, :])
+        nc.sync.dma_start(q_pool[:, 1:3, :], q_view[:, 1:3, :])
+        nc.sync.dma_start(q_pool[:, 3, :], q_view[:, 3, :])
         nc.sync.dma_start(word_pool[:], k_words[0].rearrange("p n t -> p (n t)").bitcast(I32))
         nc.vector.memset(maps[0][:, : T // 2 - 1], 0.0)
         nc.vector.memset(maps[0][:, T // 2 - 1 :], 0.0)
@@ -82,7 +83,6 @@ def tile_attend_lq_scat_topk_kernel(tc, qT, k_words, k_scales, offq, offs, out):
                 nc.sync.dma_start(k_bytes[b][:].bitcast(I32)[r:P:32, :], k_picked[:].bitcast(I32)[8 * r : P : 32, cols])
         for t in (0, 1):
             nc.scalar.activation(q_cast[t][:], q_pool[:, t, :], COPY)
-        for t in (0, 1):
             nc.scalar.activation(q_bf[:, :, t], q_cast[t][:].indirect(query_list[:]), COPY)
         for t in (2, 3):
             nc.vector.tensor_copy(q_bf[:, :, t], q_pool[:, t, :].indirect(query_list[:]))

@@ -58,8 +58,8 @@ def tile_attend_lq_scat_topk_kernel(tc, qT, k_words, k_scales, offq, offs, out):
         q_bytes = pool.tile([P, B * NQ], U8, name="q_bytes", align_bytes=64)
         links = [pool.tile([P, N], F32, name="links%d" % b) for b in range(B)]
 
-        def keys_of(b):
-            return key_list[:, b * N // 16 : (b + 1) * N // 16]
+        def keys_of(b, n0=0, n1=N):
+            return key_list[:, (b * N + n0) // 16 : (b * N + n1) // 16]
 
         def score(b, n0, n1):
             scores = psum.tile([P, n1 - n0], F32, name="scores%d_%d" % (b, n0))
@@ -89,8 +89,8 @@ def tile_attend_lq_scat_topk_kernel(tc, qT, k_words, k_scales, offq, offs, out):
         nc.vector.quantize_mx(
             out=q_codes[:].bitcast(FP8X4), scales=q_bytes[:], in_=q_bf[:].rearrange("p c t -> p (c t)")
         )
-        for b in range(B):
-            nc.vector.tensor_copy(k_codes[b][:], word_pool[:].bitcast(U32).indirect(keys_of(b)))
+        for b, n0, n1 in ((0, 0, N // 2), (0, N // 2, N), (1, 0, N)):
+            nc.vector.tensor_copy(k_codes[b][:, n0:n1], word_pool[:].bitcast(U32).indirect(keys_of(b, n0, n1)))
         for n0 in range(0, N, 128):
             score(0, n0, n0 + 128)
         score(1, 0, N)

@@ -43,10 +43,6 @@ def tile_attend_lq_scat_topk_kernel(tc, qT, k_words, k_scales, offq, offs, out):
         nc.sync.dma_start(word_pool[:], k_words[0].rearrange("p n t -> p (n t)").bitcast(I32))
         nc.vector.memset(maps[0][:, : T // 2 - 1], 0.0)
         nc.vector.memset(maps[0][:, T // 2 - 1 :], 0.0)
-        warm_in = pool.tile([P, 8], F32, name="warm_in")
-        warm_out = pool.tile([P, 8], F32, name="warm_out")
-        nc.gpsimd.memset(warm_in[:], 0.0)
-        nc.scalar.activation(warm_out[:], warm_in[:], SIGMOID)
         nc.gpsimd.memset(maps[1][:], 0.0)
 
         k_picked = pool.tile([P, B * N], U8, name="k_picked", align_bytes=64)

@@ -15,6 +15,9 @@ COPY = mybir.ActivationFunctionType.Copy
 B, NQ, N, T, D, QPOOL = 2, 128, 512, 2048, 512, 1024
 P = 128
 PACK = 4
+HALF = N // 2
+LEAD = 128
+REST = N - LEAD
 FLOPS = 2 * B * NQ * N * D
 
 
@@ -44,9 +47,11 @@ def tile_attend_lq_scat_topk_kernel(tc, qT, k_words, k_scales, offq, offs, out):
         nc.vector.memset(maps[0][:, : T // 2 - 1], 0.0)
         nc.vector.memset(maps[0][:, T // 2 - 1 :], 0.0)
         nc.gpsimd.memset(maps[1][:], 0.0)
+        zeros = pool.tile([P, LEAD], F32, name="zeros")
+        nc.gpsimd.memset(zeros[:], 0.0)
 
         k_picked = pool.tile([P, B * N], U8, name="k_picked", align_bytes=64)
-        k_bytes = [pool.tile([P, N], U8, name="k_bytes%d" % b, align_bytes=64) for b in range(B)]
+        k_bytes = pool.tile([P, B * N], U8, name="k_bytes", align_bytes=64)
         k_codes = [pool.tile([P, N], U32, name="k_codes%d" % b, align_bytes=64) for b in range(B)]
         q_cast = [pool.tile([P, QPOOL], BF16, name="q_cast%d" % t, align_bytes=64) for t in range(2)]
         q_bf = pool.tile([P, B * NQ, PACK], BF16, name="q_bf", align_bytes=64)
@@ -64,19 +69,20 @@ def tile_attend_lq_scat_topk_kernel(tc, qT, k_words, k_scales, offq, offs, out):
                 lhsT=q_codes[:, b * NQ : (b + 1) * NQ].bitcast(FP8X4),
                 lhsT_scale=q_bytes[:, b * NQ : (b + 1) * NQ],
                 rhs=k_codes[b][:, n0:n1].bitcast(FP8X4),
-                rhs_scale=k_bytes[b][:, n0:n1],
+                rhs_scale=k_bytes[:, b * N + n0 : b * N + n1],
                 start=True,
                 stop=True,
             )
             nc.scalar.activation(links[b][:, n0:n1], scores[:], SIGMOID)
 
-        for b in range(B):
-            nc.vector.tensor_copy(k_picked[:, b * N : (b + 1) * N], scale_pool[:].bitcast(U8).indirect(keys_of(b)))
-        nc.vector.tensor_copy(k_bytes[0][:].bitcast(I32), k_picked[:].bitcast(I32)[:, : N // 4])
-        for b in range(B):
-            cols = slice(b * N // 4, (b + 1) * N // 4)
-            for r in range(1 - b, 4):
-                nc.sync.dma_start(k_bytes[b][:].bitcast(I32)[r:P:32, :], k_picked[:].bitcast(I32)[8 * r : P : 32, cols])
+        for n0, n1 in ((REST, B * N), (0, REST)):
+            nc.vector.tensor_copy(k_picked[:, n0:n1], scale_pool[:].bitcast(U8).indirect(key_list[:, n0 // 16 : n1 // 16]))
+        placed, picked = k_bytes[:].bitcast(I32), k_picked[:].bitcast(I32)
+        nc.vector.tensor_copy(placed[:, REST // 4 :], picked[:, REST // 4 :])
+        for r in range(1, 4):
+            nc.sync.dma_start(placed[r:P:32, REST // 4 :], picked[8 * r : P : 32, REST // 4 :])
+        for r in range(4):
+            nc.sync.dma_start(placed[r:P:32, : REST // 4], picked[8 * r : P : 32, : REST // 4])
         for t in (0, 1):
             nc.scalar.activation(q_cast[t][:], q_pool[:, t, :], COPY)
             nc.scalar.activation(q_bf[:, :, t], q_cast[t][:].indirect(query_list[:]), COPY)
@@ -85,11 +91,18 @@ def tile_attend_lq_scat_topk_kernel(tc, qT, k_words, k_scales, offq, offs, out):
         nc.vector.quantize_mx(
             out=q_codes[:].bitcast(FP8X4), scales=q_bytes[:], in_=q_bf[:].rearrange("p c t -> p (c t)")
         )
-        for b, n0, n1 in ((0, 0, N // 2), (0, N // 2, N), (1, 0, N)):
-            nc.vector.tensor_copy(k_codes[b][:, n0:n1], word_pool[:].bitcast(U32).indirect(keys_of(b, n0, n1)))
-        for n0 in range(0, N, 128):
-            score(0, n0, n0 + 128)
-        score(1, 0, N)
-        for b in range(B):
-            nc.vector.tensor_copy(maps[b][:].indirect(keys_of(b)), links[b][:])
-            nc.sync.dma_start(out[b], maps[b][:])
+        for b, n0 in ((0, HALF), (1, 0), (1, HALF), (0, 0)):
+            nc.vector.tensor_copy(
+                k_codes[b][:, n0 : n0 + HALF], word_pool[:].bitcast(U32).indirect(keys_of(b, n0, n0 + HALF))
+            )
+        score(0, REST, N)
+        score(1, 0, HALF)
+        score(1, HALF, HALF + 128)
+        score(1, HALF + 128, N)
+        score(0, HALF, REST)
+        score(0, 0, HALF)
+        nc.vector.tensor_tensor(maps[0][:].indirect(keys_of(0, REST, N)), links[0][:, REST:], zeros[:], mybir.AluOpType.add)
+        nc.vector.tensor_copy(maps[1][:].indirect(keys_of(1)), links[1][:])
+        nc.sync.dma_start(out[1], maps[1][:])
+        nc.vector.tensor_copy(maps[0][:].indirect(keys_of(0, 0, REST)), links[0][:, :REST])
+        nc.sync.dma_start(out[0], maps[0][:])

@@ -52,7 +52,7 @@ def tile_attend_lq_scat_topk_kernel(tc, qT, k_words, k_scales, offq, offs, out):
 
         k_picked = pool.tile([P, B * N], U8, name="k_picked", align_bytes=64)
         k_bytes = pool.tile([P, B * N], U8, name="k_bytes", align_bytes=64)
-        k_codes = [pool.tile([P, N], U32, name="k_codes%d" % b, align_bytes=64) for b in range(B)]
+        k_codes = pool.tile([P, B * N], U32, name="k_codes", align_bytes=64)
         q_cast = [pool.tile([P, QPOOL], BF16, name="q_cast%d" % t, align_bytes=64) for t in range(2)]
         q_bf = pool.tile([P, B * NQ, PACK], BF16, name="q_bf", align_bytes=64)
         q_codes = pool.tile([P, B * NQ], U32, name="q_codes", align_bytes=64)
@@ -68,7 +68,7 @@ def tile_attend_lq_scat_topk_kernel(tc, qT, k_words, k_scales, offq, offs, out):
                 out=scores[:],
                 lhsT=q_codes[:, b * NQ : (b + 1) * NQ].bitcast(FP8X4),
                 lhsT_scale=q_bytes[:, b * NQ : (b + 1) * NQ],
-                rhs=k_codes[b][:, n0:n1].bitcast(FP8X4),
+                rhs=k_codes[:, b * N + n0 : b * N + n1].bitcast(FP8X4),
                 rhs_scale=k_bytes[:, b * N + n0 : b * N + n1],
                 start=True,
                 stop=True,
@@ -91,16 +91,13 @@ def tile_attend_lq_scat_topk_kernel(tc, qT, k_words, k_scales, offq, offs, out):
         nc.vector.quantize_mx(
             out=q_codes[:].bitcast(FP8X4), scales=q_bytes[:], in_=q_bf[:].rearrange("p c t -> p (c t)")
         )
-        for b, n0 in ((0, HALF), (1, 0), (1, HALF), (0, 0)):
-            nc.vector.tensor_copy(
-                k_codes[b][:, n0 : n0 + HALF], word_pool[:].bitcast(U32).indirect(keys_of(b, n0, n0 + HALF))
-            )
+        for n0, n1 in ((REST, N + HALF), (N + HALF, B * N), (0, REST)):
+            nc.vector.tensor_copy(k_codes[:, n0:n1], word_pool[:].bitcast(U32).indirect(key_list[:, n0 // 16 : n1 // 16]))
         score(0, REST, N)
         score(1, 0, HALF)
-        score(1, HALF, HALF + 128)
-        score(1, HALF + 128, N)
-        score(0, HALF, REST)
+        score(1, HALF, N)
         score(0, 0, HALF)
+        score(0, HALF, REST)
         nc.vector.tensor_tensor(maps[0][:].indirect(keys_of(0, REST, N)), links[0][:, REST:], zeros[:], mybir.AluOpType.add)
         nc.vector.tensor_copy(maps[1][:].indirect(keys_of(1)), links[1][:])
         nc.sync.dma_start(out[1], maps[1][:])

@@ -35,8 +35,7 @@ def tile_attend_lq_scat_topk_kernel(tc, qT, k_words, k_scales, offq, offs, out):
         maps = [pool.tile([P, T], F32, name="map%d" % b) for b in range(B)]
         q_view = qT.rearrange("(p t) c -> p t c", t=PACK)
 
-        nc.vector.memset(scale_pool[:, :255], 0)
-        nc.vector.memset(scale_pool[:, 255:], 0)
+        nc.vector.memset(scale_pool[:], 0)
         nc.sync.dma_start(q_pool[:, 0, :], q_view[:, 0, :])
         nc.sync.dma_start(key_list[:], offs)
         nc.sync.dma_start(query_list[:], offq)
@@ -44,11 +43,9 @@ def tile_attend_lq_scat_topk_kernel(tc, qT, k_words, k_scales, offq, offs, out):
         nc.sync.dma_start(q_pool[:, 1:3, :], q_view[:, 1:3, :])
         nc.sync.dma_start(q_pool[:, 3, :], q_view[:, 3, :])
         nc.sync.dma_start(word_pool[:], k_words[0].rearrange("p n t -> p (n t)").bitcast(I32))
-        nc.vector.memset(maps[0][:, : T // 2 - 1], 0.0)
-        nc.vector.memset(maps[0][:, T // 2 - 1 :], 0.0)
-        nc.gpsimd.memset(maps[1][:], 0.0)
         zeros = pool.tile([P, LEAD], F32, name="zeros")
-        nc.gpsimd.memset(zeros[:], 0.0)
+        for tile in maps + [zeros]:
+            nc.vector.memset(tile[:], 0.0)
 
         k_picked = pool.tile([P, B * N], U8, name="k_picked", align_bytes=64)
         k_bytes = pool.tile([P, B * N], U8, name="k_bytes", align_bytes=64)

@@ -29,74 +29,85 @@ def tile_attend_lq_scat_topk_kernel(tc, qT, k_words, k_scales, offq, offs, out):
 
         key_list = pool.tile([P, B * N // 16], U16, name="key_list")
         query_list = pool.tile([P, B * NQ // 16], U16, name="query_list")
-        scale_pool = pool.tile([P, T // 4], I32, name="scale_pool", align_bytes=64)
+        scale_pool = pool.tile([P, T // 4 + 1], I32, name="scale_pool", align_bytes=64)
         word_pool = pool.tile([P, T], I32, name="word_pool", align_bytes=64)
-        q_pool = pool.tile([P, PACK, QPOOL], F32, name="q_pool")
+        q_pool = [pool.tile([P, QPOOL], F32, name="q_pool%d" % t, align_bytes=64) for t in range(PACK)]
         maps = [pool.tile([P, T], F32, name="map%d" % b) for b in range(B)]
+        zeros = pool.tile([P, LEAD + 1], F32, name="zeros")
+        warm = pool.tile([P, 1], F32, name="warm")
         q_view = qT.rearrange("(p t) c -> p t c", t=PACK)
 
         nc.vector.memset(scale_pool[:], 0)
-        nc.sync.dma_start(q_pool[:, 0, :], q_view[:, 0, :])
+        nc.sync.dma_start(q_pool[0][:], q_view[:, 0, :])
         nc.sync.dma_start(key_list[:], offs)
+        nc.sync.dma_start(scale_pool[0:P:8, : T // 4], k_scales[0].bitcast(I32))
         nc.sync.dma_start(query_list[:], offq)
-        nc.sync.dma_start(scale_pool[0:P:8, :], k_scales[0].bitcast(I32))
-        nc.sync.dma_start(q_pool[:, 1:3, :], q_view[:, 1:3, :])
-        nc.sync.dma_start(q_pool[:, 3, :], q_view[:, 3, :])
         nc.sync.dma_start(word_pool[:], k_words[0].rearrange("p n t -> p (n t)").bitcast(I32))
-        zeros = pool.tile([P, LEAD], F32, name="zeros")
-        for tile in maps + [zeros]:
-            nc.vector.memset(tile[:], 0.0)
+        for t in range(1, PACK):
+            nc.sync.dma_start(q_pool[t][:], q_view[:, t, :])
+        nc.vector.memset(zeros[:], 0.0)
+        nc.gpsimd.memset(maps[1][:], 0.0)
+        nc.vector.memset(maps[0][:, : T - 1], 0.0)
+        nc.vector.memset(maps[0][:, T - 1 :], 0.0)
+        nc.scalar.activation(warm[:], maps[1][:, 0:1], SIGMOID)
 
         k_picked = pool.tile([P, B * N], U8, name="k_picked", align_bytes=64)
         k_bytes = pool.tile([P, B * N], U8, name="k_bytes", align_bytes=64)
-        k_codes = pool.tile([P, B * N], U32, name="k_codes", align_bytes=64)
+        k_codes = pool.tile([P, B * N - HALF], U32, name="k_codes", align_bytes=64)
         q_cast = [pool.tile([P, QPOOL], BF16, name="q_cast%d" % t, align_bytes=64) for t in range(2)]
-        q_bf = pool.tile([P, B * NQ, PACK], BF16, name="q_bf", align_bytes=64)
-        q_codes = pool.tile([P, B * NQ], U32, name="q_codes", align_bytes=64)
-        q_bytes = pool.tile([P, B * NQ], U8, name="q_bytes", align_bytes=64)
-        links = [pool.tile([P, N], F32, name="links%d" % b) for b in range(B)]
+        q_bf = [pool.tile([P, NQ, PACK], BF16, name="q_bf%d" % b, align_bytes=64) for b in range(B)]
+        q_codes = [pool.tile([P, NQ], U32, name="q_codes%d" % b, align_bytes=64) for b in range(B)]
+        q_bytes = [pool.tile([P, NQ], U8, name="q_bytes%d" % b, align_bytes=64) for b in range(B)]
+        links = [pool.tile([P, n], F32, name="links%d" % b) for b, n in enumerate((REST, N))]
 
         def keys_of(b, n0=0, n1=N):
             return key_list[:, (b * N + n0) // 16 : (b * N + n1) // 16]
 
-        def score(b, n0, n1):
+        def queries_of(b):
+            return query_list[:, b * NQ // 16 : (b + 1) * NQ // 16]
+
+        def score(b, n0, n1, codes, at):
             scores = psum.tile([P, n1 - n0], F32, name="scores%d_%d" % (b, n0))
             nc.tensor.matmul_mx(
                 out=scores[:],
-                lhsT=q_codes[:, b * NQ : (b + 1) * NQ].bitcast(FP8X4),
-                lhsT_scale=q_bytes[:, b * NQ : (b + 1) * NQ],
-                rhs=k_codes[:, b * N + n0 : b * N + n1].bitcast(FP8X4),
+                lhsT=q_codes[b][:].bitcast(FP8X4),
+                lhsT_scale=q_bytes[b][:],
+                rhs=codes.bitcast(FP8X4),
                 rhs_scale=k_bytes[:, b * N + n0 : b * N + n1],
                 start=True,
                 stop=True,
             )
-            nc.scalar.activation(links[b][:, n0:n1], scores[:], SIGMOID)
+            nc.scalar.activation(links[b][:, at : at + n1 - n0], scores[:], SIGMOID)
 
-        for n0, n1 in ((REST, B * N), (0, REST)):
-            nc.vector.tensor_copy(k_picked[:, n0:n1], scale_pool[:].bitcast(U8).indirect(key_list[:, n0 // 16 : n1 // 16]))
         placed, picked = k_bytes[:].bitcast(I32), k_picked[:].bitcast(I32)
-        nc.vector.tensor_copy(placed[:, REST // 4 :], picked[:, REST // 4 :])
-        for r in range(1, 4):
-            nc.sync.dma_start(placed[r:P:32, REST // 4 :], picked[8 * r : P : 32, REST // 4 :])
+        nc.vector.memset(placed, 0)
+        nc.vector.tensor_copy(k_picked[:], scale_pool[:, : T // 4].bitcast(U8).indirect(key_list[:]))
+        nc.scalar.activation(q_cast[0][:], q_pool[0][:], COPY)
+        for b in range(B):
+            nc.scalar.activation(q_bf[b][:, :, 0], q_cast[0][:].indirect(queries_of(b)), COPY)
         for r in range(4):
-            nc.sync.dma_start(placed[r:P:32, : REST // 4], picked[8 * r : P : 32, : REST // 4])
-        for t in (0, 1):
-            nc.scalar.activation(q_cast[t][:], q_pool[:, t, :], COPY)
-            nc.scalar.activation(q_bf[:, :, t], q_cast[t][:].indirect(query_list[:]), COPY)
-        for t in (2, 3):
-            nc.vector.tensor_copy(q_bf[:, :, t], q_pool[:, t, :].indirect(query_list[:]))
-        nc.vector.quantize_mx(
-            out=q_codes[:].bitcast(FP8X4), scales=q_bytes[:], in_=q_bf[:].rearrange("p c t -> p (c t)")
-        )
-        for n0, n1 in ((REST, N + HALF), (N + HALF, B * N), (0, REST)):
-            nc.vector.tensor_copy(k_codes[:, n0:n1], word_pool[:].bitcast(U32).indirect(key_list[:, n0 // 16 : n1 // 16]))
-        score(0, REST, N)
-        score(1, 0, HALF)
-        score(1, HALF, N)
-        score(0, 0, HALF)
-        score(0, HALF, REST)
-        nc.vector.tensor_tensor(maps[0][:].indirect(keys_of(0, REST, N)), links[0][:, REST:], zeros[:], mybir.AluOpType.add)
+            nc.scalar.dma_start(placed[r:P:32, :], picked[8 * r : P : 32, :])
+        nc.scalar.activation(q_cast[1][:], q_pool[1][:], COPY)
+        for b in reversed(range(B)):
+            nc.scalar.activation(q_bf[b][:, :, 1], q_cast[1][:].indirect(queries_of(b)), COPY)
+        nc.vector.tensor_copy(k_codes[:], word_pool[:].bitcast(U32).indirect(key_list[:, HALF // 16 :]))
+        for b in range(B):
+            nc.vector.tensor_copy(q_bf[b][:, :, 2], q_pool[2][:].indirect(queries_of(b)))
+        for b in range(B):
+            nc.vector.tensor_copy(q_bf[b][:, :, 3], q_pool[3][:].indirect(queries_of(b)))
+            nc.vector.quantize_mx(
+                out=q_codes[b][:].bitcast(FP8X4), scales=q_bytes[b][:], in_=q_bf[b][:].rearrange("p c t -> p (c t)")
+            )
+        k_late = pool.tile([P, HALF], U32, name="q_pool3", align_bytes=64)
+        nc.vector.tensor_copy(k_late[:], word_pool[:].bitcast(U32).indirect(keys_of(0, 0, HALF)))
+        score(0, REST, N, k_codes[:, REST - HALF : HALF], HALF)
+        score(1, 0, HALF, k_codes[:, HALF:N], 0)
+        score(1, HALF, N, k_codes[:, N:], HALF)
+        score(0, 0, HALF, k_late[:], 0)
+        nc.vector.tensor_tensor(maps[0][:].indirect(keys_of(0, REST, N)), links[0][:, HALF:], zeros[:, :LEAD], mybir.AluOpType.add)
+        score(0, HALF, REST, k_codes[:, : REST - HALF], HALF)
         nc.vector.tensor_copy(maps[1][:].indirect(keys_of(1)), links[1][:])
-        nc.sync.dma_start(out[1], maps[1][:])
-        nc.vector.tensor_copy(maps[0][:].indirect(keys_of(0, 0, REST)), links[0][:, :REST])
+        for half in (slice(0, T // 2), slice(T // 2, T)):
+            nc.sync.dma_start(out[1][:, half], maps[1][:, half])
+        nc.vector.tensor_copy(maps[0][:].indirect(keys_of(0, 0, REST)), links[0][:])
         nc.sync.dma_start(out[0], maps[0][:])

@@ -17,7 +17,6 @@ P = 128
 PACK = 4
 HALF = N // 2
 LEAD = 128
-REST = N - LEAD
 FLOPS = 2 * B * NQ * N * D
 
 
@@ -35,7 +34,11 @@ def tile_attend_lq_scat_topk_kernel(tc, qT, k_words, k_scales, offq, offs, out):
         maps = [pool.tile([P, T], F32, name="map%d" % b) for b in range(B)]
         zeros = pool.tile([P, LEAD + 1], F32, name="zeros")
         warm = pool.tile([P, 1], F32, name="warm")
+        k_picked = pool.tile([P, B * N], U8, name="k_picked", align_bytes=64)
+        k_bytes = pool.tile([P, B * N], U8, name="k_bytes", align_bytes=64)
+        k_codes = pool.tile([P, B * N], U32, name="k_codes", align_bytes=64)
         q_view = qT.rearrange("(p t) c -> p t c", t=PACK)
+        placed, picked = k_bytes[:].bitcast(I32), k_picked[:].bitcast(I32)
 
         nc.vector.memset(scale_pool[:], 0)
         nc.sync.dma_start(q_pool[0][:], q_view[:, 0, :])
@@ -46,68 +49,63 @@ def tile_attend_lq_scat_topk_kernel(tc, qT, k_words, k_scales, offq, offs, out):
         for t in range(1, PACK):
             nc.sync.dma_start(q_pool[t][:], q_view[:, t, :])
         nc.vector.memset(zeros[:], 0.0)
-        nc.gpsimd.memset(maps[1][:], 0.0)
-        nc.vector.memset(maps[0][:, : T - 1], 0.0)
-        nc.vector.memset(maps[0][:, T - 1 :], 0.0)
-        nc.scalar.activation(warm[:], maps[1][:, 0:1], SIGMOID)
+        nc.gpsimd.memset(placed, 0)
+        for b in range(B):
+            nc.gpsimd.memset(maps[b][:], 0.0)
+        nc.scalar.activation(warm[:], zeros[:, 0:1], SIGMOID)
 
-        k_picked = pool.tile([P, B * N], U8, name="k_picked", align_bytes=64)
-        k_bytes = pool.tile([P, B * N], U8, name="k_bytes", align_bytes=64)
-        k_codes = pool.tile([P, B * N - HALF], U32, name="k_codes", align_bytes=64)
-        q_cast = [pool.tile([P, QPOOL], BF16, name="q_cast%d" % t, align_bytes=64) for t in range(2)]
-        q_bf = [pool.tile([P, NQ, PACK], BF16, name="q_bf%d" % b, align_bytes=64) for b in range(B)]
+        q_planes = pool.tile([P, PACK, B * NQ], BF16, name="q_planes", align_bytes=64)
         q_codes = [pool.tile([P, NQ], U32, name="q_codes%d" % b, align_bytes=64) for b in range(B)]
         q_bytes = [pool.tile([P, NQ], U8, name="q_bytes%d" % b, align_bytes=64) for b in range(B)]
-        links = [pool.tile([P, n], F32, name="links%d" % b) for b, n in enumerate((REST, N))]
+        links = [pool.tile([P, N], F32, name="links%d" % b) for b in range(B)]
 
-        def keys_of(b, n0=0, n1=N):
+        def keys_of(b, n0, n1):
             return key_list[:, (b * N + n0) // 16 : (b * N + n1) // 16]
 
         def queries_of(b):
             return query_list[:, b * NQ // 16 : (b + 1) * NQ // 16]
 
-        def score(b, n0, n1, codes, at):
-            scores = psum.tile([P, n1 - n0], F32, name="scores%d_%d" % (b, n0))
-            nc.tensor.matmul_mx(
-                out=scores[:],
-                lhsT=q_codes[b][:].bitcast(FP8X4),
-                lhsT_scale=q_bytes[b][:],
-                rhs=codes.bitcast(FP8X4),
-                rhs_scale=k_bytes[:, b * N + n0 : b * N + n1],
-                start=True,
-                stop=True,
+        def quantise(b, woven):
+            nc.vector.quantize_mx(
+                out=q_codes[b][:].bitcast(FP8X4), scales=q_bytes[b][:], in_=woven[:].rearrange("p c t -> p (c t)")
             )
-            nc.scalar.activation(links[b][:, at : at + n1 - n0], scores[:], SIGMOID)
 
-        placed, picked = k_bytes[:].bitcast(I32), k_picked[:].bitcast(I32)
-        nc.vector.memset(placed, 0)
+        def score(b, cuts):
+            scores = psum.tile([P, cuts[-1] - cuts[0]], F32, name="scores%d_%d" % (b, cuts[0]))
+            for n0, n1 in zip(cuts, cuts[1:]):
+                nc.tensor.matmul_mx(
+                    out=scores[:, n0 - cuts[0] : n1 - cuts[0]],
+                    lhsT=q_codes[b][:].bitcast(FP8X4),
+                    lhsT_scale=q_bytes[b][:],
+                    rhs=k_codes[:, b * N + n0 : b * N + n1].bitcast(FP8X4),
+                    rhs_scale=k_bytes[:, b * N + n0 : b * N + n1],
+                    start=True,
+                    stop=True,
+                )
+            nc.scalar.activation(links[b][:, cuts[0] : cuts[-1]], scores[:], SIGMOID)
+
+        woven0 = pool.tile([P, NQ, PACK], BF16, name="woven", align_bytes=64)
         nc.vector.tensor_copy(k_picked[:], scale_pool[:, : T // 4].bitcast(U8).indirect(key_list[:]))
-        nc.scalar.activation(q_cast[0][:], q_pool[0][:], COPY)
-        for b in range(B):
-            nc.scalar.activation(q_bf[b][:, :, 0], q_cast[0][:].indirect(queries_of(b)), COPY)
+        nc.scalar.activation(q_planes[:, 0, :], q_pool[0][:].indirect(query_list[:]), COPY)
         for r in range(4):
             nc.scalar.dma_start(placed[r:P:32, :], picked[8 * r : P : 32, :])
-        nc.scalar.activation(q_cast[1][:], q_pool[1][:], COPY)
-        for b in reversed(range(B)):
-            nc.scalar.activation(q_bf[b][:, :, 1], q_cast[1][:].indirect(queries_of(b)), COPY)
-        nc.vector.tensor_copy(k_codes[:], word_pool[:].bitcast(U32).indirect(key_list[:, HALF // 16 :]))
+        nc.vector.tensor_copy(k_codes[:], word_pool[:].bitcast(U32).indirect(key_list[:]))
+        nc.scalar.activation(q_planes[:, 1, :], q_pool[1][:].indirect(query_list[:]), COPY)
+        nc.vector.tensor_copy(woven0[:, :, :2], q_planes[:, :2, :NQ].rearrange("p t c -> p c t"))
+        for t in range(2, PACK):
+            nc.vector.tensor_copy(woven0[:, :, t], q_pool[t][:].indirect(queries_of(0)))
+            nc.scalar.activation(q_planes[:, t, NQ:], q_pool[t][:].indirect(queries_of(1)), COPY)
+        quantise(0, woven0)
+        woven1 = pool.tile([P, NQ, PACK], BF16, name="woven", align_bytes=64)
+        nc.vector.tensor_copy(woven1[:], q_planes[:, :, NQ:].rearrange("p t c -> p c t"))
+        quantise(1, woven1)
+        score(0, (0, LEAD))
+        score(0, (LEAD, HALF, N))
+        score(1, (0, HALF))
+        score(1, (HALF, N))
+        nc.vector.tensor_tensor(maps[0][:].indirect(keys_of(0, 0, LEAD)), links[0][:, :LEAD], zeros[:, :LEAD], mybir.AluOpType.add)
+        nc.vector.tensor_copy(maps[0][:].indirect(keys_of(0, LEAD, N)), links[0][:, LEAD:])
+        for n0 in (0, HALF):
+            nc.scalar.activation(maps[1][:].indirect(keys_of(1, n0, n0 + HALF)), links[1][:, n0 : n0 + HALF], COPY)
         for b in range(B):
-            nc.vector.tensor_copy(q_bf[b][:, :, 2], q_pool[2][:].indirect(queries_of(b)))
-        for b in range(B):
-            nc.vector.tensor_copy(q_bf[b][:, :, 3], q_pool[3][:].indirect(queries_of(b)))
-            nc.vector.quantize_mx(
-                out=q_codes[b][:].bitcast(FP8X4), scales=q_bytes[b][:], in_=q_bf[b][:].rearrange("p c t -> p (c t)")
-            )
-        k_late = pool.tile([P, HALF], U32, name="q_pool3", align_bytes=64)
-        nc.vector.tensor_copy(k_late[:], word_pool[:].bitcast(U32).indirect(keys_of(0, 0, HALF)))
-        score(0, REST, N, k_codes[:, REST - HALF : HALF], HALF)
-        score(1, 0, HALF, k_codes[:, HALF:N], 0)
-        score(1, HALF, N, k_codes[:, N:], HALF)
-        score(0, 0, HALF, k_late[:], 0)
-        nc.vector.tensor_tensor(maps[0][:].indirect(keys_of(0, REST, N)), links[0][:, HALF:], zeros[:, :LEAD], mybir.AluOpType.add)
-        score(0, HALF, REST, k_codes[:, : REST - HALF], HALF)
-        nc.vector.tensor_copy(maps[1][:].indirect(keys_of(1)), links[1][:])
-        for half in (slice(0, T // 2), slice(T // 2, T)):
-            nc.sync.dma_start(out[1][:, half], maps[1][:, half])
-        nc.vector.tensor_copy(maps[0][:].indirect(keys_of(0, 0, REST)), links[0][:])
-        nc.sync.dma_start(out[0], maps[0][:])
+            nc.sync.dma_start(out[b], maps[b][:])

@@ -16,7 +16,7 @@ B, NQ, N, T, D, QPOOL = 2, 128, 512, 2048, 512, 1024
 P = 128
 PACK = 4
 HALF = N // 2
-LEAD = 128
+LEAD = 64
 FLOPS = 2 * B * NQ * N * D
 
 
@@ -49,9 +49,9 @@ def tile_attend_lq_scat_topk_kernel(tc, qT, k_words, k_scales, offq, offs, out):
         for t in range(1, PACK):
             nc.sync.dma_start(q_pool[t][:], q_view[:, t, :])
         nc.vector.memset(zeros[:], 0.0)
-        nc.gpsimd.memset(placed, 0)
         for b in range(B):
             nc.gpsimd.memset(maps[b][:], 0.0)
+        nc.gpsimd.memset(placed, 0)
         nc.scalar.activation(warm[:], zeros[:, 0:1], SIGMOID)
 
         q_planes = pool.tile([P, PACK, B * NQ], BF16, name="q_planes", align_bytes=64)
@@ -100,7 +100,8 @@ def tile_attend_lq_scat_topk_kernel(tc, qT, k_words, k_scales, offq, offs, out):
         nc.vector.tensor_copy(woven1[:], q_planes[:, :, NQ:].rearrange("p t c -> p c t"))
         quantise(1, woven1)
         score(0, (0, LEAD))
-        score(0, (LEAD, HALF, N))
+        score(0, (LEAD, 2 * LEAD, HALF))
+        score(0, (HALF, N))
         score(1, (0, HALF))
         score(1, (HALF, N))
         nc.vector.tensor_tensor(maps[0][:].indirect(keys_of(0, 0, LEAD)), links[0][:, :LEAD], zeros[:, :LEAD], mybir.AluOpType.add)

from contextlib import ExitStack

import concourse.mybir as mybir

F32 = mybir.dt.float32
BF16 = mybir.dt.bfloat16
I32 = mybir.dt.int32
U32 = mybir.dt.uint32
U16 = mybir.dt.uint16
U8 = mybir.dt.uint8
FP8X4 = mybir.dt.float8_e4m3fn_x4
SIGMOID = mybir.ActivationFunctionType.Sigmoid
COPY = mybir.ActivationFunctionType.Copy

B, NQ, N, T, D, QPOOL = 2, 128, 512, 2048, 512, 1024
P = 128
PACK = 4
HALF = N // 2
LEAD = 64
FLOPS = 2 * B * NQ * N * D


def tile_attend_lq_scat_topk_kernel(tc, qT, k_words, k_scales, offq, offs, out):
    nc = tc.nc
    with ExitStack() as ctx:
        pool = ctx.enter_context(tc.tile_pool(name="held", bufs=1))
        psum = ctx.enter_context(tc.psum_pool(name="psum", bufs=1))

        key_list = pool.tile([P, B * N // 16], U16, name="key_list")
        query_list = pool.tile([P, B * NQ // 16], U16, name="query_list")
        scale_pool = pool.tile([P, T // 4 + 1], I32, name="scale_pool", align_bytes=64)
        word_pool = pool.tile([P, T], I32, name="word_pool", align_bytes=64)
        q_pool = [pool.tile([P, QPOOL], F32, name="q_pool%d" % t, align_bytes=64) for t in range(PACK)]
        maps = [pool.tile([P, T], F32, name="map%d" % b) for b in range(B)]
        zeros = pool.tile([P, LEAD + 1], F32, name="zeros")
        warm = pool.tile([P, 1], F32, name="warm")
        k_picked = pool.tile([P, B * N], U8, name="k_picked", align_bytes=64)
        k_bytes = pool.tile([P, B * N], U8, name="k_bytes", align_bytes=64)
        k_codes = pool.tile([P, B * N], U32, name="k_codes", align_bytes=64)
        q_view = qT.rearrange("(p t) c -> p t c", t=PACK)
        placed, picked = k_bytes[:].bitcast(I32), k_picked[:].bitcast(I32)

        nc.vector.memset(scale_pool[:], 0)
        nc.sync.dma_start(q_pool[0][:], q_view[:, 0, :])
        nc.sync.dma_start(key_list[:], offs)
        nc.sync.dma_start(scale_pool[0:P:8, : T // 4], k_scales[0].bitcast(I32))
        nc.sync.dma_start(query_list[:], offq)
        nc.sync.dma_start(word_pool[:], k_words[0].rearrange("p n t -> p (n t)").bitcast(I32))
        for t in range(1, PACK):
            nc.sync.dma_start(q_pool[t][:], q_view[:, t, :])
        nc.vector.memset(zeros[:], 0.0)
        for b in range(B):
            nc.gpsimd.memset(maps[b][:], 0.0)
        nc.gpsimd.memset(placed, 0)
        nc.scalar.activation(warm[:], zeros[:, 0:1], SIGMOID)

        q_planes = pool.tile([P, PACK, B * NQ], BF16, name="q_planes", align_bytes=64)
        q_codes = [pool.tile([P, NQ], U32, name="q_codes%d" % b, align_bytes=64) for b in range(B)]
        q_bytes = [pool.tile([P, NQ], U8, name="q_bytes%d" % b, align_bytes=64) for b in range(B)]
        links = [pool.tile([P, N], F32, name="links%d" % b) for b in range(B)]

        def keys_of(b, n0, n1):
            return key_list[:, (b * N + n0) // 16 : (b * N + n1) // 16]

        def queries_of(b):
            return query_list[:, b * NQ // 16 : (b + 1) * NQ // 16]

        def quantise(b, woven):
            nc.vector.quantize_mx(
                out=q_codes[b][:].bitcast(FP8X4), scales=q_bytes[b][:], in_=woven[:].rearrange("p c t -> p (c t)")
            )

        def score(b, cuts):
            scores = psum.tile([P, cuts[-1] - cuts[0]], F32, name="scores%d_%d" % (b, cuts[0]))
            for n0, n1 in zip(cuts, cuts[1:]):
                nc.tensor.matmul_mx(
                    out=scores[:, n0 - cuts[0] : n1 - cuts[0]],
                    lhsT=q_codes[b][:].bitcast(FP8X4),
                    lhsT_scale=q_bytes[b][:],
                    rhs=k_codes[:, b * N + n0 : b * N + n1].bitcast(FP8X4),
                    rhs_scale=k_bytes[:, b * N + n0 : b * N + n1],
                    start=True,
                    stop=True,
                )
            nc.scalar.activation(links[b][:, cuts[0] : cuts[-1]], scores[:], SIGMOID)

        woven0 = pool.tile([P, NQ, PACK], BF16, name="woven", align_bytes=64)
        nc.vector.tensor_copy(k_picked[:], scale_pool[:, : T // 4].bitcast(U8).indirect(key_list[:]))
        nc.scalar.activation(q_planes[:, 0, :], q_pool[0][:].indirect(query_list[:]), COPY)
        for r in range(4):
            nc.scalar.dma_start(placed[r:P:32, :], picked[8 * r : P : 32, :])
        nc.vector.tensor_copy(k_codes[:], word_pool[:].bitcast(U32).indirect(key_list[:]))
        nc.scalar.activation(q_planes[:, 1, :], q_pool[1][:].indirect(query_list[:]), COPY)
        nc.vector.tensor_copy(woven0[:, :, :2], q_planes[:, :2, :NQ].rearrange("p t c -> p c t"))
        for t in range(2, PACK):
            nc.vector.tensor_copy(woven0[:, :, t], q_pool[t][:].indirect(queries_of(0)))
            nc.scalar.activation(q_planes[:, t, NQ:], q_pool[t][:].indirect(queries_of(1)), COPY)
        quantise(0, woven0)
        woven1 = pool.tile([P, NQ, PACK], BF16, name="woven", align_bytes=64)
        nc.vector.tensor_copy(woven1[:], q_planes[:, :, NQ:].rearrange("p t c -> p c t"))
        quantise(1, woven1)
        score(0, (0, LEAD))
        score(0, (LEAD, 2 * LEAD, HALF))
        score(0, (HALF, N))
        score(1, (0, HALF))
        score(1, (HALF, N))
        nc.vector.tensor_tensor(maps[0][:].indirect(keys_of(0, 0, LEAD)), links[0][:, :LEAD], zeros[:, :LEAD], mybir.AluOpType.add)
        nc.vector.tensor_copy(maps[0][:].indirect(keys_of(0, LEAD, N)), links[0][:, LEAD:])
        for n0 in (0, HALF):
            nc.scalar.activation(maps[1][:].indirect(keys_of(1, n0, n0 + HALF)), links[1][:, n0 : n0 + HALF], COPY)
        for b in range(B):
            nc.sync.dma_start(out[b], maps[b][:])
